import numpy as np
import ml_dtypes


def mxq(x, axis, fmt="e4m3"):
    dtype, down = {"e4m3": (ml_dtypes.float8_e4m3fn, 7), "e5m2": (ml_dtypes.float8_e5m2, 14)}[fmt]
    v = np.moveaxis(np.asarray(x, np.float32).astype(ml_dtypes.bfloat16).astype(np.float64), axis, -1)
    blocks = v.reshape(v.shape[:-1] + (-1, 32))
    amax = np.abs(blocks).max(-1, keepdims=True)
    byte = np.maximum(np.where(amax > 0, np.frexp(amax)[1] - 1 + 127, 0) - down, 1)
    scale = np.exp2(byte - 127.0)
    codes = (blocks / scale).astype(np.float32).astype(dtype).astype(np.float64)
    return np.moveaxis((codes * scale).reshape(v.shape), -1, axis)


WIDE = False


def mx_kscale(k):
    if not WIDE:
        return np.ones(k)
    levels = np.array([10, -10, 5, -5, 0])
    if k % 512:
        return np.exp2(np.random.permutation(np.resize(levels, k // 32))).repeat(32)
    a = np.empty((k // 512, 16))
    for p in range(k // 512):
        a[p, :8] = np.random.permutation(np.resize(levels, 8))
        for g in range(8):
            far = levels[np.abs(levels - a[p, g]) >= 10]
            a[p, g + 8] = far[np.random.randint(len(far))]
    return np.exp2(a.ravel()).repeat(32)


def f64(x):
    return np.asarray(x).astype(np.float64)


def striped(idx):
    return np.tile(idx.reshape(-1, 16).T, (8, 1)).astype(np.uint16)


def unstriped(offs):
    return offs[:16].T.reshape(-1).astype(np.int64)


def striped8(idx):
    return np.concatenate([x.reshape(-1, 16).T for x in idx]).astype(np.uint16)


def runs(offs, k):
    lists = np.stack([offs[16 * r : 16 * r + 16].T.reshape(-1) for r in range(8)]).astype(np.int64)
    return lists[np.arange(k) % 512 // 64]


def pack_weight(w):
    k, n = w.shape
    w = f64(np.asarray(w, np.float32).astype(ml_dtypes.bfloat16)).reshape(k // 32, 32, n)
    amax = np.abs(w).max(1)
    byte = np.clip(np.where(amax > 0, np.frexp(amax)[1] - 1 + 127 - 7, 1), 1, 254)
    scaled = (w * np.exp2(127.0 - byte)[:, None, :]).reshape(k, n).astype(np.float32)
    words = np.ascontiguousarray(scaled.reshape(k // 512, 128, 4, n).transpose(0, 1, 3, 2)).astype(ml_dtypes.float8_e4m3fn).view(np.uint8)
    return words, np.ascontiguousarray(byte.astype(np.uint8).reshape(k // 512, 16, n))


def unpack_weight(words, scales):
    g, p, n, _ = words.shape
    vals = np.ascontiguousarray(words).view(ml_dtypes.float8_e4m3fn).astype(np.float64) * np.repeat(np.exp2(scales.astype(np.float64) - 127.0), 8, axis=1)[..., None]
    return vals.transpose(0, 1, 3, 2).reshape(g * 512, n)


E2M1 = np.array([0.0, 0.5, 1.0, 1.5, 2.0, 3.0, 4.0, 6.0, -0.0, -0.5, -1.0, -1.5, -2.0, -3.0, -4.0, -6.0])


def pack_fp4(w):
    k, n = w.shape
    w = f64(np.asarray(w, np.float32).astype(ml_dtypes.bfloat16)).reshape(k // 32, 32, n)
    amax = np.abs(w).max(1)
    mant, ex = np.frexp(amax / 6.0)
    byte = np.clip(np.where(amax > 0, np.where(mant > 0.5, ex, ex - 1) + 127, 1), 1, 254)
    scaled = (w * np.exp2(127.0 - byte)[:, None, :]).reshape(k, n).astype(np.float32)
    c = np.ascontiguousarray(scaled.reshape(k // 512, 128, 4, n).transpose(0, 1, 3, 2)).astype(ml_dtypes.float4_e2m1fn).view(np.uint8) & 0xF
    words = (c[..., 0::2] | (c[..., 1::2] << 4)).reshape(k // 512, 128, 2 * n)
    return np.ascontiguousarray(words), np.ascontiguousarray(byte.astype(np.uint8).reshape(k // 512, 16, n))


def unpack_fp4(words, scales):
    g, _, n = scales.shape
    words = np.ascontiguousarray(words).reshape(g, 128, n, 2)
    nib = np.empty((g, 128, n, 4), np.uint8)
    nib[..., 0::2] = words & 0xF
    nib[..., 1::2] = words >> 4
    vals = E2M1[nib] * np.repeat(np.exp2(scales.astype(np.float64) - 127.0), 8, axis=1)[..., None]
    return vals.transpose(0, 1, 3, 2).reshape(g * 512, n)


def relu(v):
    return np.maximum(v, 0.0)

def planes(y):
    n, m = y.shape
    v = y.astype(np.float32).astype(ml_dtypes.bfloat16).astype(np.float64).reshape(n // 32, 32, m)
    top = np.abs(v).max(1)
    byte = np.clip(np.where(top > 0, np.frexp(top)[1] - 1 + 127 - 7, 1), 1, 254)
    codes = (v * np.exp2(127.0 - byte)[:, None, :]).reshape(n, m).astype(np.float32).astype(ml_dtypes.float8_e4m3fn).view(np.uint8)
    words = codes.reshape(n // 512, 128, 4, m).transpose(0, 1, 3, 2)
    return np.ascontiguousarray(words), np.ascontiguousarray(byte.astype(np.uint8).reshape(n // 512, 16, m))


K, T, S, H, C = 512, 2048, 512, 512, 512


def setup_inputs():
    n = np.random.standard_normal
    s = mx_kscale(K)[:, None]
    packed_xT = pack_weight(n((K, T)) * s)
    packed_w1 = pack_fp4(n((K, H)) / np.sqrt(K) / s)
    return {
        "x_words": packed_xT[0],
        "x_scales": packed_xT[1],
        "w1_words": packed_w1[0],
        "w1_scales": packed_w1[1],
        "gs": (np.random.uniform(0.5, 1.5, (K, 1)) / s).astype(np.float32),
        "gs2": (np.random.uniform(0.5, 1.5, (K, 1)) / s).astype(np.float32),
        "offs": striped(np.random.permutation(T)[:S]),
        "n1": striped8(np.stack([np.random.permutation(S) for _ in range(8)])),
        "n2": striped8(np.stack([np.random.permutation(S) for _ in range(8)])),
        "n3": striped(np.random.permutation(S)),
        "ca": striped(np.random.permutation(T)[:C]),
        "cb": striped(np.random.permutation(T)[:C]),
        "n4": striped(np.random.permutation(S)),
        "n5": striped(np.random.permutation(S)),
    }


def reference(x_words, x_scales, w1_words, w1_scales, gs, gs2, offs, n1, n2, n3, ca, cb, n4, n5):
    x_ca = unpack_weight(x_words, x_scales)[:, unstriped(ca)]
    xq = unpack_weight(x_words, x_scales)[:, unstriped(offs)]
    y = unpack_fp4(w1_words, w1_scales).T @ xq
    sq = (y) ** 2
    z = f64(gs) * ((y[np.arange(H)[:, None], runs(n2, H)]) / (np.sqrt(sq + sq[np.arange(H)[:, None], runs(n1, H)] + 0.25)))
    a = 0.0625 * ((x_ca.T @ mxq(z, 0, "e4m3")))
    x_cb = unpack_weight(x_words, x_scales)[:, unstriped(cb)]
    rl = relu(y)
    ds = np.zeros((H, S))
    ds[:, unstriped(n3)] = rl
    z2 = f64(gs2) * (ds - (0.5 * y))
    b = 0.0625 * ((x_cb.T @ mxq(z2, 0, "e4m3")))
    out_0 = a[:, unstriped(n4)] - (np.tanh(b) * b[:, unstriped(n5)])
    return (out_0,) + planes(out_0)

@@ -1,0 +1,200 @@
+from contextlib import ExitStack
+
+import concourse.mybir as mybir
+
+F32 = mybir.dt.float32
+BF16 = mybir.dt.bfloat16
+I32 = mybir.dt.int32
+U32 = mybir.dt.uint32
+U16 = mybir.dt.uint16
+U8 = mybir.dt.uint8
+FP8X4 = mybir.dt.float8_e4m3fn_x4
+FP4X4 = mybir.dt.float4_e2m1fn_x4
+ALU = mybir.AluOpType
+ACT = mybir.ActivationFunctionType
+
+P = 128
+T = 2048
+S = 512
+PACK = 4
+HALF = S // 2
+FLOPS = 3 * 2 * 512 * 512 * 512
+
+
+def tile_picked_twocdsoftbrmssend_none_po_kernel(
+    tc, x_words, x_scales, w1_words, w1_scales, gs, gs2, offs, n1, n2, n3, ca, cb, n4, n5, out_0, out_1, out_2
+):
+    nc = tc.nc
+    with ExitStack() as ctx:
+        held = ctx.enter_context(tc.tile_pool(name="held", bufs=1))
+        psum = ctx.enter_context(tc.psum_pool(name="psum", bufs=1))
+
+        def sbuf(name, width, dtype):
+            return held.tile([P, width], dtype, name=name, align_bytes=64)
+
+        def load_list(name, src):
+            tile = held.tile([P, S // 16], U16, name=name)
+            nc.sync.dma_start(tile[:], src)
+            return tile
+
+        def load_scale_rows(queues, tile, src):
+            for q in range(4):
+                queues[q].dma_start(tile[32 * q : 32 * q + 4, :].bitcast(I32), src[0, 4 * q : 4 * q + 4, :].bitcast(I32))
+
+        x_w = sbuf("x_w", T, U32)
+        x_s = sbuf("x_s", T, U8)
+        w_w = sbuf("w_w", 2 * S, U8)
+        w_s = sbuf("w_s", S, U8)
+        nc.gpsimd.memset(x_s[:].bitcast(I32), 0)
+        nc.vector.memset(w_s[:].bitcast(I32), 0)
+        l_offs = load_list("l_offs", offs)
+        nc.scalar.dma_start(w_w[:].bitcast(I32), w1_words[0].bitcast(I32))
+        nc.sync.dma_start(x_w[:].bitcast(I32), x_words[0].rearrange("p c r -> p (c r)").bitcast(I32))
+        load_scale_rows([nc.sync] * 4, x_s, x_scales)
+        load_scale_rows([nc.scalar] * 3 + [nc.gpsimd], w_s, w1_scales)
+        l_cb = load_list("l_cb", cb)
+        g1 = sbuf("g1", PACK, F32)
+        g2 = sbuf("g2", PACK, F32)
+        nc.gpsimd.dma_start(g2[:], gs2.rearrange("(p t) o -> p (t o)", t=PACK))
+        l_n3 = load_list("l_n3", n3)
+        l_ca = load_list("l_ca", ca)
+        nc.gpsimd.dma_start(g1[:], gs.rearrange("(p t) o -> p (t o)", t=PACK))
+        l_n1 = load_list("l_n1", n1)
+        l_n2 = load_list("l_n2", n2)
+        l_n5 = load_list("l_n5", n5)
+        l_n4 = load_list("l_n4", n4)
+
+        wd_w = sbuf("wd_w", 2 * S, U8)
+        wd_s = sbuf("wd_s", S, U8)
+        q_w = sbuf("q_w", S, U32)
+        q_s = sbuf("q_s", S, U8)
+        nc.vector.tensor_copy(
+            wd_w[:].rearrange("p (t m b) -> p t m b", t=PACK, b=2), w_w[:].rearrange("p (m t b) -> p t m b", t=PACK, b=2)
+        )
+        nc.vector.tensor_copy(q_s[:], x_s[:].indirect(l_offs[:]))
+        nc.vector.tensor_copy(q_w[:], x_w[:].indirect(l_offs[:]))
+        nc.vector.tensor_copy(wd_s[:].rearrange("p (t m) -> p t m", t=PACK), w_s[:].rearrange("p (m t) -> p t m", t=PACK))
+        g2n = sbuf("g2n", PACK, F32)
+        nc.gpsimd.tensor_scalar(g2n[:], g2[:], -0.5, 0.0, ALU.mult, ALU.add)
+
+        y = [psum.tile([P, S], F32, name=f"y{t}", tag=f"ya{t}") for t in range(PACK)]
+        for t in range(PACK):
+            nc.tensor.matmul_mx(
+                out=y[t][:], lhsT=wd_w[:, 2 * P * t : 2 * P * (t + 1)].bitcast(FP4X4), lhsT_scale=wd_s[:, P * t : P * (t + 1)],
+                rhs=q_w[:].bitcast(FP8X4), rhs_scale=q_s[:], start=True, stop=True,
+            )
+
+        def gather_scales(name, lst):
+            plain = sbuf(name + "_plain", S, U8)
+            dealt = sbuf(name, S, U8)
+            nc.vector.tensor_copy(plain[:], x_s[:].indirect(lst[:]))
+            nc.vector.tensor_copy(dealt[:].rearrange("p (t m) -> p t m", t=PACK), plain[:].rearrange("p (m t) -> p t m", t=PACK))
+            return dealt
+
+        def gather_words(name, lst):
+            dealt = sbuf(name, S, U32)
+            nc.vector.tensor_copy(dealt[:].rearrange("p (t m) -> p m t", t=PACK), x_w[:].indirect(lst[:]))
+            return dealt
+
+        cb_s = gather_scales("cb_s", l_cb)
+        cb_w = gather_words("cb_w", l_cb)
+
+        sqw = [sbuf(f"sqw{t}", 2 * S, F32) for t in range(PACK)]
+        ygw = [sbuf(f"ygw{t}", 2 * S, F32) for t in range(PACK)]
+        ds = [sbuf(f"ds{t}", S if t else 2 * S, F32) for t in range(PACK)]
+        d = sbuf("d", PACK * S, F32)
+        r = sbuf("r", PACK * S, F32)
+        z = sbuf("z", PACK * S, F32)
+        z2 = sbuf("z2", PACK * S, BF16)
+
+        def plane(tile, t):
+            return tile[:, S * t : S * (t + 1)]
+
+        for t in range(PACK):
+            nc.vector.tensor_scalar(sqw[t][:, S:], y[t][:], 0.0, g2[:, t : t + 1], ALU.max, ALU.mult)
+            nc.scalar.activation(sqw[t][:, :S], y[t][:], ACT.Square)
+            nc.sync.dma_start(ygw[t][:, S:], sqw[t][:, :S])
+
+        def scatter_scalar(t):
+            for h in range(2):
+                nc.scalar.activation(
+                    ds[t][:].indirect(l_n3[:, 16 * h : 16 * (h + 1)]), sqw[t][:, S + HALF * h : S + HALF * (h + 1)], ACT.Copy
+                )
+
+        scatter_scalar(1)
+        nc.vector.tensor_copy(ds[0][:].indirect(l_n3[:]), sqw[0][:, S:])
+        scatter_scalar(2)
+        for t in range(PACK):
+            nc.vector.tensor_tensor(plane(d, t), sqw[t][:].indirect(l_n1[:]), ygw[t][:, S:], ALU.add)
+        scatter_scalar(3)
+        ca_s = gather_scales("ca_s", l_ca)
+        ca_w = gather_words("ca_w", l_ca)
+        for t in range(PACK):
+            nc.vector.scalar_tensor_tensor(plane(z2, t), y[t][:], g2n[:, t : t + 1], ds[t][:, :S], ALU.mult, ALU.add)
+        for t in range(PACK):
+            nc.scalar.activation(ygw[t][:, :S], y[t][:], ACT.Copy, scale=g1[:, t : t + 1])
+            nc.scalar.activation(plane(r, t), plane(d, t), ACT.Abs_reciprocal_sqrt, bias=0.25)
+
+        def weave(copy, name, planes, cols):
+            woven = sbuf(name, PACK * (cols.stop - cols.start), BF16)
+            src = planes[:].rearrange("p (t c) -> p t c", t=PACK)[:, :, cols]
+            copy(woven[:].rearrange("p (c i t) -> p c t i", i=4, t=PACK), src.rearrange("p t (c i) -> p c t i", i=4))
+            return woven
+
+        def quantise(name, planes):
+            woven = weave(nc.vector.tensor_copy, name + "_woven", planes, slice(0, S))
+            words = sbuf(name + "_w", S, U32)
+            scales = sbuf(name + "_s", S, U8)
+            nc.vector.quantize_mx(out=words[:].bitcast(FP8X4), scales=scales[:], in_=woven[:])
+            return words, scales
+
+        def product(banks, lw, ls, rw, rs):
+            for t in range(PACK):
+                nc.tensor.matmul_mx(
+                    out=banks[t][:], lhsT=lw[:, P * t : P * (t + 1)].bitcast(FP8X4), lhsT_scale=ls[:, P * t : P * (t + 1)],
+                    rhs=rw[:].bitcast(FP8X4), rhs_scale=rs[:], start=True, stop=True,
+                )
+
+        z2_w, z2_s = quantise("z2q", z2)
+        b = [psum.tile([P, S], F32, name=f"b{t}") for t in range(PACK)]
+        product(b, cb_w, cb_s, z2_w, z2_s)
+        for t in range(PACK):
+            nc.vector.tensor_tensor(plane(z, t), ygw[t][:].indirect(l_n2[:]), plane(r, t), ALU.mult)
+        z_w, z_s = quantise("zq", z)
+        a = [psum.tile([P, S], F32, name=f"a{t}", tag=f"ya{t}") for t in range(PACK)]
+        product(a, ca_w, ca_s, z_w, z_s)
+
+        bw = [sbuf(f"bw{t}", S, F32) for t in range(PACK)]
+        aw = [sbuf(f"aw{t}", S, F32) for t in range(PACK)]
+        th = sbuf("th", PACK * S, F32)
+        m = sbuf("m", PACK * S, F32)
+        o = sbuf("o", PACK * S, F32)
+        for t in range(PACK):
+            nc.scalar.activation(bw[t][:], b[t][:], ACT.Copy, scale=0.0625)
+            nc.scalar.activation(plane(th, t), b[t][:], ACT.Tanh, scale=0.0625)
+        for t in range(PACK):
+            nc.scalar.activation(aw[t][:], a[t][:], ACT.Copy, scale=0.0625)
+        for t in range(PACK):
+            for h in range(2):
+                cols = slice(S * t + HALF * h, S * t + HALF * (h + 1))
+                nc.vector.tensor_tensor(m[:, cols], bw[t][:].indirect(l_n5[:, 16 * h : 16 * (h + 1)]), th[:, cols], ALU.mult)
+        out_rows = out_0.rearrange("(p t) j -> p t j", t=PACK)
+        o_w = sbuf("o_w", S, U32)
+        o_s = sbuf("o_s", S, U8)
+        ga = sbuf("ga", PACK * HALF, F32)
+        for h in range(2):
+            half = slice(HALF * h, HALF * (h + 1))
+            for t in range(PACK):
+                cols = slice(S * t + HALF * h, S * t + HALF * (h + 1))
+                picked = aw[t][:].indirect(l_n4[:, 16 * h : 16 * (h + 1)])
+                if h == 0:
+                    nc.scalar.activation(ga[:, HALF * t : HALF * (t + 1)], picked, ACT.Copy)
+                    picked = ga[:, HALF * t : HALF * (t + 1)]
+                nc.vector.tensor_tensor(o[:, cols], picked, m[:, cols], ALU.subtract)
+            nc.sync.dma_start(out_rows[:, :, half], o[:].rearrange("p (t c) -> p t c", t=PACK)[:, :, half])
+            woven = weave(nc.scalar.copy if h == 0 else nc.vector.tensor_copy, f"o_woven{h}", o, half)
+            nc.vector.quantize_mx(out=o_w[:, half].bitcast(FP8X4), scales=o_s[:, half], in_=woven[:])
+            nc.sync.dma_start(out_1[0, :, half, :].rearrange("p c r -> p (c r)").bitcast(I32), o_w[:, half].bitcast(I32))
+        for q in range(4):
+            queue = nc.scalar if q < 3 else nc.sync
+            queue.dma_start(out_2[0, 4 * q : 4 * q + 4, :].bitcast(I32), o_s[32 * q : 32 * q + 4, :].bitcast(I32))

@@ -50,8 +50,8 @@ def tile_picked_twocdsoftbrmssend_none_po_kernel(
         l_offs = load_list("l_offs", offs)
         nc.scalar.dma_start(w_w[:].bitcast(I32), w1_words[0].bitcast(I32))
         nc.sync.dma_start(x_w[:].bitcast(I32), x_words[0].rearrange("p c r -> p (c r)").bitcast(I32))
-        load_scale_rows([nc.sync] * 4, x_s, x_scales)
-        load_scale_rows([nc.scalar] * 3 + [nc.gpsimd], w_s, w1_scales)
+        load_scale_rows([nc.scalar] * 4, x_s, x_scales)
+        load_scale_rows([nc.sync] * 3 + [nc.gpsimd], w_s, w1_scales)
         l_cb = load_list("l_cb", cb)
         g1 = sbuf("g1", PACK, F32)
         g2 = sbuf("g2", PACK, F32)
@@ -64,6 +64,9 @@ def tile_picked_twocdsoftbrmssend_none_po_kernel(
         l_n5 = load_list("l_n5", n5)
         l_n4 = load_list("l_n4", n4)
 
+        warm = sbuf("warm", 8, F32)
+        nc.vector.memset(warm[:], 1.0)
+        nc.scalar.activation(warm[:, 4:5], warm[:, 0:1], ACT.Abs_reciprocal_sqrt, bias=0.25)
         wd_w = sbuf("wd_w", 2 * S, U8)
         wd_s = sbuf("wd_s", S, U8)
         q_w = sbuf("q_w", S, U32)
@@ -84,60 +87,58 @@ def tile_picked_twocdsoftbrmssend_none_po_kernel(
                 rhs=q_w[:].bitcast(FP8X4), rhs_scale=q_s[:], start=True, stop=True,
             )
 
-        def gather_scales(name, lst):
-            plain = sbuf(name + "_plain", S, U8)
+        def gather_scales(name, lst, tag):
+            plain = held.tile([P, S], U8, name=name + "_plain", tag=tag, align_bytes=64)
             dealt = sbuf(name, S, U8)
             nc.vector.tensor_copy(plain[:], x_s[:].indirect(lst[:]))
             nc.vector.tensor_copy(dealt[:].rearrange("p (t m) -> p t m", t=PACK), plain[:].rearrange("p (m t) -> p t m", t=PACK))
             return dealt
 
-        def gather_words(name, lst):
-            dealt = sbuf(name, S, U32)
+        def gather_words(name, lst, tag):
+            dealt = held.tile([P, S], U32, name=name, tag=tag, align_bytes=64)
             nc.vector.tensor_copy(dealt[:].rearrange("p (t m) -> p m t", t=PACK), x_w[:].indirect(lst[:]))
             return dealt
 
-        cb_s = gather_scales("cb_s", l_cb)
-        cb_w = gather_words("cb_w", l_cb)
-
-        sqw = [sbuf(f"sqw{t}", 2 * S, F32) for t in range(PACK)]
+        sqw = [sbuf(f"sqw{t}", S, F32) for t in range(PACK)]
         ygw = [sbuf(f"ygw{t}", 2 * S, F32) for t in range(PACK)]
-        ds = [sbuf(f"ds{t}", S if t else 2 * S, F32) for t in range(PACK)]
-        d = sbuf("d", PACK * S, F32)
-        r = sbuf("r", PACK * S, F32)
-        z = sbuf("z", PACK * S, F32)
-        z2 = sbuf("z2", PACK * S, BF16)
+        r_all = sbuf("r_all", PACK * S, F32)
+        ds = [sbuf(f"ds{t}", S, F32) for t in range(PACK)]
+        sq2 = sbuf("sq2", PACK * S, F32)
+        rl = [ygw[PACK - 1 - t][:, :S] for t in range(PACK)]
 
         def plane(tile, t):
             return tile[:, S * t : S * (t + 1)]
 
-        for t in range(PACK):
-            nc.vector.tensor_scalar(sqw[t][:, S:], y[t][:], 0.0, g2[:, t : t + 1], ALU.max, ALU.mult)
-            nc.scalar.activation(sqw[t][:, :S], y[t][:], ACT.Square)
-            nc.sync.dma_start(ygw[t][:, S:], sqw[t][:, :S])
+        def half_plane(tile, t, h):
+            return tile[:, S * t + HALF * h : S * t + HALF * (h + 1)]
 
-        def scatter_scalar(t):
+        for t in range(PACK):
+            nc.scalar.activation(sqw[t][:], y[t][:], ACT.Square)
+            nc.vector.tensor_scalar(rl[t], y[t][:], 0.0, g2[:, t : t + 1], ALU.max, ALU.mult)
+            nc.sync.dma_start(plane(sq2, t), sqw[t][:])
+        cb_s = gather_scales("cb_s", l_cb, "g2")
+        ca_s = gather_scales("ca_s", l_ca, "g2")
+        cb_w = gather_words("cb_w", l_cb, "cb_w")
+        ca_w = gather_words("ca_w", l_ca, "q_w")
+        for h in range(2):
+            for t in range(PACK):
+                nc.scalar.activation(ds[t][:].indirect(l_n3[:, 16 * h : 16 * (h + 1)]), half_plane(rl[t], 0, h), ACT.Copy)
+        for t in range(PACK):
             for h in range(2):
-                nc.scalar.activation(
-                    ds[t][:].indirect(l_n3[:, 16 * h : 16 * (h + 1)]), sqw[t][:, S + HALF * h : S + HALF * (h + 1)], ACT.Copy
+                nc.vector.tensor_tensor(
+                    half_plane(ygw[t], 1, h), sqw[t][:].indirect(l_n1[:, 16 * h : 16 * (h + 1)]), half_plane(sq2, t, h), ALU.add
                 )
-
-        scatter_scalar(1)
-        nc.vector.tensor_copy(ds[0][:].indirect(l_n3[:]), sqw[0][:, S:])
-        scatter_scalar(2)
+        z2 = held.tile([P, PACK * S], BF16, name="z2", tag="sq2", align_bytes=64)
         for t in range(PACK):
-            nc.vector.tensor_tensor(plane(d, t), sqw[t][:].indirect(l_n1[:]), ygw[t][:, S:], ALU.add)
-        scatter_scalar(3)
-        ca_s = gather_scales("ca_s", l_ca)
-        ca_w = gather_words("ca_w", l_ca)
-        for t in range(PACK):
-            nc.vector.scalar_tensor_tensor(plane(z2, t), y[t][:], g2n[:, t : t + 1], ds[t][:, :S], ALU.mult, ALU.add)
+            nc.vector.scalar_tensor_tensor(plane(z2, t), y[t][:], g2n[:, t : t + 1], ds[t][:], ALU.mult, ALU.add)
+        r = [plane(r_all, t) for t in range(PACK)]
         for t in range(PACK):
             nc.scalar.activation(ygw[t][:, :S], y[t][:], ACT.Copy, scale=g1[:, t : t + 1])
-            nc.scalar.activation(plane(r, t), plane(d, t), ACT.Abs_reciprocal_sqrt, bias=0.25)
+            nc.scalar.activation(r[t], ygw[t][:, S:], ACT.Abs_reciprocal_sqrt, bias=0.25)
 
         def weave(copy, name, planes, cols):
             woven = sbuf(name, PACK * (cols.stop - cols.start), BF16)
-            src = planes[:].rearrange("p (t c) -> p t c", t=PACK)[:, :, cols]
+            src = planes.rearrange("p (t c) -> p t c", t=PACK)[:, :, cols]
             copy(woven[:].rearrange("p (c i t) -> p c t i", i=4, t=PACK), src.rearrange("p t (c i) -> p c t i", i=4))
             return woven
 
@@ -155,29 +156,27 @@ def tile_picked_twocdsoftbrmssend_none_po_kernel(
                     rhs=rw[:].bitcast(FP8X4), rhs_scale=rs[:], start=True, stop=True,
                 )
 
-        z2_w, z2_s = quantise("z2q", z2)
+        z2_w, z2_s = quantise("z2q", z2[:])
         b = [psum.tile([P, S], F32, name=f"b{t}") for t in range(PACK)]
         product(b, cb_w, cb_s, z2_w, z2_s)
+        z = held.tile([P, PACK * S], F32, name="z", tag="z2q_woven", align_bytes=64)
         for t in range(PACK):
-            nc.vector.tensor_tensor(plane(z, t), ygw[t][:].indirect(l_n2[:]), plane(r, t), ALU.mult)
-        z_w, z_s = quantise("zq", z)
+            nc.vector.tensor_tensor(plane(z, t), ygw[t][:].indirect(l_n2[:]), r[t], ALU.mult)
+        z_w, z_s = quantise("zq", z[:])
         a = [psum.tile([P, S], F32, name=f"a{t}", tag=f"ya{t}") for t in range(PACK)]
         product(a, ca_w, ca_s, z_w, z_s)
 
-        bw = [sbuf(f"bw{t}", S, F32) for t in range(PACK)]
         aw = [sbuf(f"aw{t}", S, F32) for t in range(PACK)]
         th = sbuf("th", PACK * S, F32)
-        m = sbuf("m", PACK * S, F32)
+        m = held.tile([P, PACK * S], F32, name="m", tag="zq_woven", align_bytes=64)
         o = sbuf("o", PACK * S, F32)
         for t in range(PACK):
-            nc.scalar.activation(bw[t][:], b[t][:], ACT.Copy, scale=0.0625)
+            nc.scalar.activation(ygw[t][:, :S], b[t][:], ACT.Copy, scale=0.0625)
             nc.scalar.activation(plane(th, t), b[t][:], ACT.Tanh, scale=0.0625)
         for t in range(PACK):
             nc.scalar.activation(aw[t][:], a[t][:], ACT.Copy, scale=0.0625)
         for t in range(PACK):
-            for h in range(2):
-                cols = slice(S * t + HALF * h, S * t + HALF * (h + 1))
-                nc.vector.tensor_tensor(m[:, cols], bw[t][:].indirect(l_n5[:, 16 * h : 16 * (h + 1)]), th[:, cols], ALU.mult)
+            nc.vector.tensor_tensor(plane(m, t), ygw[t][:].indirect(l_n5[:]), plane(th, t), ALU.mult)
         out_rows = out_0.rearrange("(p t) j -> p t j", t=PACK)
         o_w = sbuf("o_w", S, U32)
         o_s = sbuf("o_s", S, U8)
@@ -187,12 +186,18 @@ def tile_picked_twocdsoftbrmssend_none_po_kernel(
             for t in range(PACK):
                 cols = slice(S * t + HALF * h, S * t + HALF * (h + 1))
                 picked = aw[t][:].indirect(l_n4[:, 16 * h : 16 * (h + 1)])
-                if h == 0:
+                if h == 1:
                     nc.scalar.activation(ga[:, HALF * t : HALF * (t + 1)], picked, ACT.Copy)
                     picked = ga[:, HALF * t : HALF * (t + 1)]
                 nc.vector.tensor_tensor(o[:, cols], picked, m[:, cols], ALU.subtract)
             nc.sync.dma_start(out_rows[:, :, half], o[:].rearrange("p (t c) -> p t c", t=PACK)[:, :, half])
-            woven = weave(nc.scalar.copy if h == 0 else nc.vector.tensor_copy, f"o_woven{h}", o, half)
+        o_woven = [
+            weave(copy, f"o_woven{h}", o[:], slice(HALF * h, HALF * (h + 1)))
+            for h, copy in enumerate((nc.scalar.copy, nc.vector.tensor_copy))
+        ]
+        for h in range(2):
+            half = slice(HALF * h, HALF * (h + 1))
+            woven = o_woven[h]
             nc.vector.quantize_mx(out=o_w[:, half].bitcast(FP8X4), scales=o_s[:, half], in_=woven[:])
             nc.sync.dma_start(out_1[0, :, half, :].rearrange("p c r -> p (c r)").bitcast(I32), o_w[:, half].bitcast(I32))
         for q in range(4):

@@ -18,6 +18,7 @@ T = 2048
 S = 512
 PACK = 4
 HALF = S // 2
+FUSED = 2
 FLOPS = 3 * 2 * 512 * 512 * 512
 
 
@@ -75,8 +76,8 @@ def tile_picked_twocdsoftbrmssend_none_po_kernel(
             wd_w[:].rearrange("p (t m b) -> p t m b", t=PACK, b=2), w_w[:].rearrange("p (m t b) -> p t m b", t=PACK, b=2)
         )
         nc.vector.tensor_copy(q_s[:], x_s[:].indirect(l_offs[:]))
-        nc.vector.tensor_copy(q_w[:], x_w[:].indirect(l_offs[:]))
         nc.vector.tensor_copy(wd_s[:].rearrange("p (t m) -> p t m", t=PACK), w_s[:].rearrange("p (m t) -> p t m", t=PACK))
+        nc.vector.tensor_copy(q_w[:], x_w[:].indirect(l_offs[:]))
         g2n = sbuf("g2n", PACK, F32)
         nc.gpsimd.tensor_scalar(g2n[:], g2[:], -0.5, 0.0, ALU.mult, ALU.add)
 
@@ -116,12 +117,13 @@ def tile_picked_twocdsoftbrmssend_none_po_kernel(
             nc.scalar.activation(sqw[t][:], y[t][:], ACT.Square)
             nc.vector.tensor_scalar(rl[t], y[t][:], 0.0, g2[:, t : t + 1], ALU.max, ALU.mult)
             nc.sync.dma_start(plane(sq2, t), sqw[t][:])
-        cb_s = gather_scales("cb_s", l_cb, "g2")
+        nc.vector.tensor_copy(ds[3][:].indirect(l_n3[:, 0:16]), half_plane(rl[3], 0, 0))
+        cb_s = gather_scales("cb_s", l_cb, "cb_plain")
         ca_s = gather_scales("ca_s", l_ca, "g2")
         cb_w = gather_words("cb_w", l_cb, "cb_w")
         ca_w = gather_words("ca_w", l_ca, "q_w")
         for h in range(2):
-            for t in range(PACK):
+            for t in range(PACK if h else PACK - 1):
                 nc.scalar.activation(ds[t][:].indirect(l_n3[:, 16 * h : 16 * (h + 1)]), half_plane(rl[t], 0, h), ACT.Copy)
         for t in range(PACK):
             for h in range(2):
@@ -136,14 +138,12 @@ def tile_picked_twocdsoftbrmssend_none_po_kernel(
             nc.scalar.activation(ygw[t][:, :S], y[t][:], ACT.Copy, scale=g1[:, t : t + 1])
             nc.scalar.activation(r[t], ygw[t][:, S:], ACT.Abs_reciprocal_sqrt, bias=0.25)
 
-        def weave(copy, name, planes, cols):
-            woven = sbuf(name, PACK * (cols.stop - cols.start), BF16)
+        def weave(copy, woven, planes, cols):
             src = planes.rearrange("p (t c) -> p t c", t=PACK)[:, :, cols]
-            copy(woven[:].rearrange("p (c i t) -> p c t i", i=4, t=PACK), src.rearrange("p t (c i) -> p c t i", i=4))
-            return woven
+            dst = woven[:, PACK * cols.start : PACK * cols.stop]
+            copy(dst.rearrange("p (c i t) -> p c t i", i=4, t=PACK), src.rearrange("p t (c i) -> p c t i", i=4))
 
-        def quantise(name, planes):
-            woven = weave(nc.vector.tensor_copy, name + "_woven", planes, slice(0, S))
+        def quantise(name, woven):
             words = sbuf(name + "_w", S, U32)
             scales = sbuf(name + "_s", S, U8)
             nc.vector.quantize_mx(out=words[:].bitcast(FP8X4), scales=scales[:], in_=woven[:])
@@ -156,23 +156,31 @@ def tile_picked_twocdsoftbrmssend_none_po_kernel(
                     rhs=rw[:].bitcast(FP8X4), rhs_scale=rs[:], start=True, stop=True,
                 )
 
-        z2_w, z2_s = quantise("z2q", z2[:])
+        z2_woven = sbuf("z2_woven", PACK * S, BF16)
+        weave(nc.vector.tensor_copy, z2_woven, z2[:], slice(0, S))
+        z2_w, z2_s = quantise("z2q", z2_woven)
         b = [psum.tile([P, S], F32, name=f"b{t}") for t in range(PACK)]
         product(b, cb_w, cb_s, z2_w, z2_s)
-        z = held.tile([P, PACK * S], F32, name="z", tag="z2q_woven", align_bytes=64)
+        z = held.tile([P, PACK * S], F32, name="z", tag="sq2", align_bytes=64)
         for t in range(PACK):
             nc.vector.tensor_tensor(plane(z, t), ygw[t][:].indirect(l_n2[:]), r[t], ALU.mult)
-        z_w, z_s = quantise("zq", z[:])
+        th = sbuf("th", PACK * S, F32)
+
+        def leave_b(t):
+            nc.scalar.activation(ygw[t][:, :S], b[t][:], ACT.Copy, scale=0.0625)
+            nc.scalar.activation(plane(th, t), b[t][:], ACT.Tanh, scale=0.0625)
+
+        z_woven = sbuf("z_woven", PACK * S, BF16)
+        weave(nc.vector.tensor_copy, z_woven, z[:], slice(0, S))
+        for t in range(PACK):
+            leave_b(t)
+        z_w, z_s = quantise("zq", z_woven)
         a = [psum.tile([P, S], F32, name=f"a{t}", tag=f"ya{t}") for t in range(PACK)]
         product(a, ca_w, ca_s, z_w, z_s)
 
         aw = [sbuf(f"aw{t}", S, F32) for t in range(PACK)]
-        th = sbuf("th", PACK * S, F32)
-        m = held.tile([P, PACK * S], F32, name="m", tag="zq_woven", align_bytes=64)
+        m = held.tile([P, PACK * S], F32, name="m", tag="sq2", align_bytes=64)
         o = sbuf("o", PACK * S, F32)
-        for t in range(PACK):
-            nc.scalar.activation(ygw[t][:, :S], b[t][:], ACT.Copy, scale=0.0625)
-            nc.scalar.activation(plane(th, t), b[t][:], ACT.Tanh, scale=0.0625)
         for t in range(PACK):
             nc.scalar.activation(aw[t][:], a[t][:], ACT.Copy, scale=0.0625)
         for t in range(PACK):
@@ -180,25 +188,23 @@ def tile_picked_twocdsoftbrmssend_none_po_kernel(
         out_rows = out_0.rearrange("(p t) j -> p t j", t=PACK)
         o_w = sbuf("o_w", S, U32)
         o_s = sbuf("o_s", S, U8)
-        ga = sbuf("ga", PACK * HALF, F32)
+        ga = sbuf("ga", PACK * S, F32)
         for h in range(2):
             half = slice(HALF * h, HALF * (h + 1))
             for t in range(PACK):
                 cols = slice(S * t + HALF * h, S * t + HALF * (h + 1))
                 picked = aw[t][:].indirect(l_n4[:, 16 * h : 16 * (h + 1)])
-                if h == 1:
-                    nc.scalar.activation(ga[:, HALF * t : HALF * (t + 1)], picked, ACT.Copy)
-                    picked = ga[:, HALF * t : HALF * (t + 1)]
+                if PACK * h + t >= FUSED:
+                    nc.scalar.activation(ga[:, cols], picked, ACT.Copy)
+                    picked = ga[:, cols]
                 nc.vector.tensor_tensor(o[:, cols], picked, m[:, cols], ALU.subtract)
-            nc.sync.dma_start(out_rows[:, :, half], o[:].rearrange("p (t c) -> p t c", t=PACK)[:, :, half])
-        o_woven = [
-            weave(copy, f"o_woven{h}", o[:], slice(HALF * h, HALF * (h + 1)))
-            for h, copy in enumerate((nc.scalar.copy, nc.vector.tensor_copy))
-        ]
+                nc.sync.dma_start(out_rows[:, t, half], o[:, cols])
+        o_woven = sbuf("o_woven", PACK * S, BF16)
+        weave(nc.scalar.copy, o_woven, o[:], slice(0, HALF))
+        weave(nc.vector.tensor_copy, o_woven, o[:], slice(HALF, S))
         for h in range(2):
             half = slice(HALF * h, HALF * (h + 1))
-            woven = o_woven[h]
-            nc.vector.quantize_mx(out=o_w[:, half].bitcast(FP8X4), scales=o_s[:, half], in_=woven[:])
+            nc.vector.quantize_mx(out=o_w[:, half].bitcast(FP8X4), scales=o_s[:, half], in_=o_woven[:, PACK * half.start : PACK * half.stop])
             nc.sync.dma_start(out_1[0, :, half, :].rearrange("p c r -> p (c r)").bitcast(I32), o_w[:, half].bitcast(I32))
         for q in range(4):
             queue = nc.scalar if q < 3 else nc.sync

@@ -17,9 +17,12 @@ P = 128
 T = 2048
 S = 512
 PACK = 4
+QUADRANTS = 4
+PER_COLUMN = 16
 HALF = S // 2
-FUSED = 2
-FLOPS = 3 * 2 * 512 * 512 * 512
+VECTOR_SCATTER = 256
+FUSED_HALVES = 2
+FLOPS = 3 * 2 * S * S * S
 
 
 def tile_picked_twocdsoftbrmssend_none_po_kernel(
@@ -30,17 +33,68 @@ def tile_picked_twocdsoftbrmssend_none_po_kernel(
         held = ctx.enter_context(tc.tile_pool(name="held", bufs=1))
         psum = ctx.enter_context(tc.psum_pool(name="psum", bufs=1))
 
-        def sbuf(name, width, dtype):
-            return held.tile([P, width], dtype, name=name, align_bytes=64)
+        def sbuf(name, width, dtype, tag=None):
+            return held.tile([P, width], dtype, name=name, tag=tag or name, align_bytes=64)
 
         def load_list(name, src):
-            tile = held.tile([P, S // 16], U16, name=name)
+            tile = held.tile([P, S // PER_COLUMN], U16, name=name)
             nc.sync.dma_start(tile[:], src)
             return tile
 
+        def entries(list_tile, cols):
+            return list_tile[:, cols.start // PER_COLUMN : cols.stop // PER_COLUMN]
+
         def load_scale_rows(queues, tile, src):
-            for q in range(4):
+            for q in range(QUADRANTS):
                 queues[q].dma_start(tile[32 * q : 32 * q + 4, :].bitcast(I32), src[0, 4 * q : 4 * q + 4, :].bitcast(I32))
+
+        def plane(tile, t, cols=slice(0, S)):
+            return tile[:, S * t + cols.start : S * t + cols.stop]
+
+        def deal_scales(dealt, plain):
+            nc.vector.tensor_copy(
+                dealt[:].rearrange("p (t m) -> p t m", t=PACK), plain[:].rearrange("p (m t) -> p t m", t=PACK)
+            )
+
+        def gather_scales(name, list_tile, tag):
+            plain = sbuf(name + "_plain", S, U8, tag)
+            dealt = sbuf(name, S, U8)
+            nc.vector.tensor_copy(plain[:], x_s[:].indirect(list_tile[:]))
+            deal_scales(dealt, plain)
+            return dealt
+
+        def gather_words(name, list_tile, tag):
+            dealt = sbuf(name, S, U32, tag)
+            nc.vector.tensor_copy(dealt[:].rearrange("p (t m) -> p m t", t=PACK), x_w[:].indirect(list_tile[:]))
+            return dealt
+
+        def weave(copy, woven, planes, cols):
+            src = planes[:].rearrange("p (t c) -> p t c", t=PACK)[:, :, cols]
+            dst = woven[:, PACK * cols.start : PACK * cols.stop]
+            copy(dst.rearrange("p (c i t) -> p c t i", i=4, t=PACK), src.rearrange("p t (c i) -> p c t i", i=4))
+
+        def quantise(name, woven):
+            words = sbuf(name + "_w", S, U32)
+            scales = sbuf(name + "_s", S, U8)
+            nc.vector.quantize_mx(out=words[:].bitcast(FP8X4), scales=scales[:], in_=woven[:])
+            return words, scales
+
+        def product(banks, lhs_slices, lhs_scales, rhs_words, rhs_scales):
+            for t in range(PACK):
+                nc.tensor.matmul_mx(
+                    out=banks[t][:],
+                    lhsT=lhs_slices[t],
+                    lhsT_scale=lhs_scales[:, P * t : P * (t + 1)],
+                    rhs=rhs_words[:].bitcast(FP8X4),
+                    rhs_scale=rhs_scales[:],
+                    start=True,
+                    stop=True,
+                )
+
+        def fp8_slices(words):
+            return [words[:, P * t : P * (t + 1)].bitcast(FP8X4) for t in range(PACK)]
+
+        halves = [slice(0, HALF), slice(HALF, S)]
 
         x_w = sbuf("x_w", T, U32)
         x_s = sbuf("x_s", T, U8)
@@ -52,7 +106,7 @@ def tile_picked_twocdsoftbrmssend_none_po_kernel(
         nc.scalar.dma_start(w_w[:].bitcast(I32), w1_words[0].bitcast(I32))
         nc.sync.dma_start(x_w[:].bitcast(I32), x_words[0].rearrange("p c r -> p (c r)").bitcast(I32))
         load_scale_rows([nc.scalar] * 4, x_s, x_scales)
-        load_scale_rows([nc.sync] * 3 + [nc.gpsimd], w_s, w1_scales)
+        load_scale_rows([nc.sync, nc.sync, nc.sync, nc.gpsimd], w_s, w1_scales)
         l_cb = load_list("l_cb", cb)
         g1 = sbuf("g1", PACK, F32)
         g2 = sbuf("g2", PACK, F32)
@@ -68,144 +122,100 @@ def tile_picked_twocdsoftbrmssend_none_po_kernel(
         warm = sbuf("warm", 8, F32)
         nc.vector.memset(warm[:], 1.0)
         nc.scalar.activation(warm[:, 4:5], warm[:, 0:1], ACT.Abs_reciprocal_sqrt, bias=0.25)
+
         wd_w = sbuf("wd_w", 2 * S, U8)
         wd_s = sbuf("wd_s", S, U8)
         q_w = sbuf("q_w", S, U32)
         q_s = sbuf("q_s", S, U8)
         nc.vector.tensor_copy(
-            wd_w[:].rearrange("p (t m b) -> p t m b", t=PACK, b=2), w_w[:].rearrange("p (m t b) -> p t m b", t=PACK, b=2)
+            wd_w[:].rearrange("p (t m e) -> p t m e", t=PACK, e=2), w_w[:].rearrange("p (m t e) -> p t m e", t=PACK, e=2)
         )
         nc.vector.tensor_copy(q_s[:], x_s[:].indirect(l_offs[:]))
-        nc.vector.tensor_copy(wd_s[:].rearrange("p (t m) -> p t m", t=PACK), w_s[:].rearrange("p (m t) -> p t m", t=PACK))
+        deal_scales(wd_s, w_s)
         nc.vector.tensor_copy(q_w[:], x_w[:].indirect(l_offs[:]))
-        g2n = sbuf("g2n", PACK, F32)
-        nc.gpsimd.tensor_scalar(g2n[:], g2[:], -0.5, 0.0, ALU.mult, ALU.add)
-
+        g2_half = sbuf("g2_half", PACK, F32)
+        nc.gpsimd.tensor_scalar(g2_half[:], g2[:], -0.5, 0.0, ALU.mult, ALU.add)
         y = [psum.tile([P, S], F32, name=f"y{t}", tag=f"ya{t}") for t in range(PACK)]
+        product(y, [wd_w[:, 2 * P * t : 2 * P * (t + 1)].bitcast(FP4X4) for t in range(PACK)], wd_s, q_w, q_s)
+
+        sq_win = [sbuf(f"sq_win{t}", 2 * S, F32) for t in range(PACK)]
+        y_win = [sbuf(f"y_win{t}", 2 * S, F32) for t in range(PACK)]
+        sq_copy = sbuf("sq_copy", PACK * S, F32, "chain")
         for t in range(PACK):
-            nc.tensor.matmul_mx(
-                out=y[t][:], lhsT=wd_w[:, 2 * P * t : 2 * P * (t + 1)].bitcast(FP4X4), lhsT_scale=wd_s[:, P * t : P * (t + 1)],
-                rhs=q_w[:].bitcast(FP8X4), rhs_scale=q_s[:], start=True, stop=True,
-            )
+            nc.scalar.activation(plane(sq_win[t], 0), y[t][:], ACT.Square)
+            nc.vector.tensor_scalar(plane(sq_win[t], 1), y[t][:], 0.0, g2[:, t : t + 1], ALU.max, ALU.mult)
+            nc.sync.dma_start(plane(sq_copy, t), plane(sq_win[t], 0))
 
-        def gather_scales(name, lst, tag):
-            plain = held.tile([P, S], U8, name=name + "_plain", tag=tag, align_bytes=64)
-            dealt = sbuf(name, S, U8)
-            nc.vector.tensor_copy(plain[:], x_s[:].indirect(lst[:]))
-            nc.vector.tensor_copy(dealt[:].rearrange("p (t m) -> p t m", t=PACK), plain[:].rearrange("p (m t) -> p t m", t=PACK))
-            return dealt
-
-        def gather_words(name, lst, tag):
-            dealt = held.tile([P, S], U32, name=name, tag=tag, align_bytes=64)
-            nc.vector.tensor_copy(dealt[:].rearrange("p (t m) -> p m t", t=PACK), x_w[:].indirect(lst[:]))
-            return dealt
-
-        sqw = [sbuf(f"sqw{t}", S, F32) for t in range(PACK)]
-        ygw = [sbuf(f"ygw{t}", 2 * S, F32) for t in range(PACK)]
-        r_all = sbuf("r_all", PACK * S, F32)
         ds = [sbuf(f"ds{t}", S, F32) for t in range(PACK)]
-        sq2 = sbuf("sq2", PACK * S, F32)
-        rl = [ygw[PACK - 1 - t][:, :S] for t in range(PACK)]
-
-        def plane(tile, t):
-            return tile[:, S * t : S * (t + 1)]
-
-        def half_plane(tile, t, h):
-            return tile[:, S * t + HALF * h : S * t + HALF * (h + 1)]
-
-        for t in range(PACK):
-            nc.scalar.activation(sqw[t][:], y[t][:], ACT.Square)
-            nc.vector.tensor_scalar(rl[t], y[t][:], 0.0, g2[:, t : t + 1], ALU.max, ALU.mult)
-            nc.sync.dma_start(plane(sq2, t), sqw[t][:])
-        nc.vector.tensor_copy(ds[3][:].indirect(l_n3[:, 0:16]), half_plane(rl[3], 0, 0))
+        last = PACK - 1
+        head, rest = slice(0, VECTOR_SCATTER), slice(VECTOR_SCATTER, S)
+        nc.vector.tensor_copy(ds[last][:].indirect(entries(l_n3, head)), plane(sq_win[last], 1, head))
         cb_s = gather_scales("cb_s", l_cb, "cb_plain")
         ca_s = gather_scales("ca_s", l_ca, "g2")
         cb_w = gather_words("cb_w", l_cb, "cb_w")
         ca_w = gather_words("ca_w", l_ca, "q_w")
-        for h in range(2):
-            for t in range(PACK if h else PACK - 1):
-                nc.scalar.activation(ds[t][:].indirect(l_n3[:, 16 * h : 16 * (h + 1)]), half_plane(rl[t], 0, h), ACT.Copy)
-        for t in range(PACK):
-            for h in range(2):
-                nc.vector.tensor_tensor(
-                    half_plane(ygw[t], 1, h), sqw[t][:].indirect(l_n1[:, 16 * h : 16 * (h + 1)]), half_plane(sq2, t, h), ALU.add
-                )
-        z2 = held.tile([P, PACK * S], BF16, name="z2", tag="sq2", align_bytes=64)
-        for t in range(PACK):
-            nc.vector.scalar_tensor_tensor(plane(z2, t), y[t][:], g2n[:, t : t + 1], ds[t][:], ALU.mult, ALU.add)
-        r = [plane(r_all, t) for t in range(PACK)]
-        for t in range(PACK):
-            nc.scalar.activation(ygw[t][:, :S], y[t][:], ACT.Copy, scale=g1[:, t : t + 1])
-            nc.scalar.activation(r[t], ygw[t][:, S:], ACT.Abs_reciprocal_sqrt, bias=0.25)
+        for t, cols in [(t, cols) for cols in halves for t in range(last)] + [(last, rest)]:
+            nc.scalar.activation(ds[t][:].indirect(entries(l_n3, cols)), plane(sq_win[t], 1, cols), ACT.Copy)
 
-        def weave(copy, woven, planes, cols):
-            src = planes.rearrange("p (t c) -> p t c", t=PACK)[:, :, cols]
-            dst = woven[:, PACK * cols.start : PACK * cols.stop]
-            copy(dst.rearrange("p (c i t) -> p c t i", i=4, t=PACK), src.rearrange("p t (c i) -> p c t i", i=4))
+        for t in range(PACK):
+            nc.vector.tensor_tensor(plane(y_win[t], 1), sq_win[t][:].indirect(l_n1[:]), plane(sq_copy, t), ALU.add)
 
-        def quantise(name, woven):
-            words = sbuf(name + "_w", S, U32)
-            scales = sbuf(name + "_s", S, U8)
-            nc.vector.quantize_mx(out=words[:].bitcast(FP8X4), scales=scales[:], in_=woven[:])
-            return words, scales
-
-        def product(banks, lw, ls, rw, rs):
-            for t in range(PACK):
-                nc.tensor.matmul_mx(
-                    out=banks[t][:], lhsT=lw[:, P * t : P * (t + 1)].bitcast(FP8X4), lhsT_scale=ls[:, P * t : P * (t + 1)],
-                    rhs=rw[:].bitcast(FP8X4), rhs_scale=rs[:], start=True, stop=True,
-                )
+        z2 = sbuf("z2", PACK * S, BF16, "chain")
+        for t in range(PACK):
+            nc.vector.scalar_tensor_tensor(plane(z2, t), y[t][:], g2_half[:, t : t + 1], ds[t][:], ALU.mult, ALU.add)
+        inv_root = sbuf("inv_root", PACK * S, F32)
+        for t in range(PACK):
+            nc.scalar.activation(plane(inv_root, t), plane(y_win[t], 1), ACT.Abs_reciprocal_sqrt, bias=0.25)
+        for t in range(PACK):
+            nc.scalar.activation(plane(y_win[t], 0), y[t][:], ACT.Copy, scale=g1[:, t : t + 1])
 
         z2_woven = sbuf("z2_woven", PACK * S, BF16)
-        weave(nc.vector.tensor_copy, z2_woven, z2[:], slice(0, S))
-        z2_w, z2_s = quantise("z2q", z2_woven)
+        weave(nc.vector.tensor_copy, z2_woven, z2, slice(0, S))
+        z2_w, z2_s = quantise("z2", z2_woven)
         b = [psum.tile([P, S], F32, name=f"b{t}") for t in range(PACK)]
-        product(b, cb_w, cb_s, z2_w, z2_s)
-        z = held.tile([P, PACK * S], F32, name="z", tag="sq2", align_bytes=64)
+        product(b, fp8_slices(cb_w), cb_s, z2_w, z2_s)
+
+        z = sbuf("z", PACK * S, F32, "chain")
         for t in range(PACK):
-            nc.vector.tensor_tensor(plane(z, t), ygw[t][:].indirect(l_n2[:]), r[t], ALU.mult)
-        th = sbuf("th", PACK * S, F32)
-
-        def leave_b(t):
-            nc.scalar.activation(ygw[t][:, :S], b[t][:], ACT.Copy, scale=0.0625)
-            nc.scalar.activation(plane(th, t), b[t][:], ACT.Tanh, scale=0.0625)
-
+            nc.vector.tensor_tensor(plane(z, t), y_win[t][:].indirect(l_n2[:]), plane(inv_root, t), ALU.mult)
+        tanh_b = sbuf("tanh_b", PACK * S, F32)
         z_woven = sbuf("z_woven", PACK * S, BF16)
-        weave(nc.vector.tensor_copy, z_woven, z[:], slice(0, S))
+        weave(nc.vector.tensor_copy, z_woven, z, slice(0, S))
         for t in range(PACK):
-            leave_b(t)
-        z_w, z_s = quantise("zq", z_woven)
+            nc.scalar.activation(plane(y_win[t], 0), b[t][:], ACT.Copy, scale=0.0625)
+            nc.scalar.activation(plane(tanh_b, t), b[t][:], ACT.Tanh, scale=0.0625)
+        z_w, z_s = quantise("z", z_woven)
         a = [psum.tile([P, S], F32, name=f"a{t}", tag=f"ya{t}") for t in range(PACK)]
-        product(a, ca_w, ca_s, z_w, z_s)
+        product(a, fp8_slices(ca_w), ca_s, z_w, z_s)
 
-        aw = [sbuf(f"aw{t}", S, F32) for t in range(PACK)]
-        m = held.tile([P, PACK * S], F32, name="m", tag="sq2", align_bytes=64)
-        o = sbuf("o", PACK * S, F32)
+        a_win = [sbuf(f"a_win{t}", S, F32) for t in range(PACK)]
+        tanh_b_prod = sbuf("tanh_b_prod", PACK * S, F32, "chain")
+        result = sbuf("result", PACK * S, F32)
         for t in range(PACK):
-            nc.scalar.activation(aw[t][:], a[t][:], ACT.Copy, scale=0.0625)
+            nc.scalar.activation(a_win[t][:], a[t][:], ACT.Copy, scale=0.0625)
         for t in range(PACK):
-            nc.vector.tensor_tensor(plane(m, t), ygw[t][:].indirect(l_n5[:]), plane(th, t), ALU.mult)
+            nc.vector.tensor_tensor(plane(tanh_b_prod, t), y_win[t][:].indirect(l_n5[:]), plane(tanh_b, t), ALU.mult)
+
         out_rows = out_0.rearrange("(p t) j -> p t j", t=PACK)
         o_w = sbuf("o_w", S, U32)
         o_s = sbuf("o_s", S, U8)
-        ga = sbuf("ga", PACK * S, F32)
-        for h in range(2):
-            half = slice(HALF * h, HALF * (h + 1))
+        a_picked = sbuf("a_picked", PACK * S, F32)
+        for h, cols in enumerate(halves):
             for t in range(PACK):
-                cols = slice(S * t + HALF * h, S * t + HALF * (h + 1))
-                picked = aw[t][:].indirect(l_n4[:, 16 * h : 16 * (h + 1)])
-                if PACK * h + t >= FUSED:
-                    nc.scalar.activation(ga[:, cols], picked, ACT.Copy)
-                    picked = ga[:, cols]
-                nc.vector.tensor_tensor(o[:, cols], picked, m[:, cols], ALU.subtract)
-                nc.sync.dma_start(out_rows[:, t, half], o[:, cols])
+                picked = a_win[t][:].indirect(entries(l_n4, cols))
+                if PACK * h + t >= FUSED_HALVES:
+                    nc.scalar.activation(plane(a_picked, t, cols), picked, ACT.Copy)
+                    picked = plane(a_picked, t, cols)
+                nc.vector.tensor_tensor(plane(result, t, cols), picked, plane(tanh_b_prod, t, cols), ALU.subtract)
+                nc.sync.dma_start(out_rows[:, t, cols], plane(result, t, cols))
+
         o_woven = sbuf("o_woven", PACK * S, BF16)
-        weave(nc.scalar.copy, o_woven, o[:], slice(0, HALF))
-        weave(nc.vector.tensor_copy, o_woven, o[:], slice(HALF, S))
-        for h in range(2):
-            half = slice(HALF * h, HALF * (h + 1))
-            nc.vector.quantize_mx(out=o_w[:, half].bitcast(FP8X4), scales=o_s[:, half], in_=o_woven[:, PACK * half.start : PACK * half.stop])
-            nc.sync.dma_start(out_1[0, :, half, :].rearrange("p c r -> p (c r)").bitcast(I32), o_w[:, half].bitcast(I32))
-        for q in range(4):
-            queue = nc.scalar if q < 3 else nc.sync
+        weave(nc.scalar.copy, o_woven, result, halves[0])
+        weave(nc.vector.tensor_copy, o_woven, result, halves[1])
+        for cols in halves:
+            nc.vector.quantize_mx(
+                out=o_w[:, cols].bitcast(FP8X4), scales=o_s[:, cols], in_=o_woven[:, PACK * cols.start : PACK * cols.stop]
+            )
+            nc.sync.dma_start(out_1[0, :, cols, :].rearrange("p c r -> p (c r)").bitcast(I32), o_w[:, cols].bitcast(I32))
+        for q, queue in enumerate([nc.scalar, nc.scalar, nc.scalar, nc.sync]):
             queue.dma_start(out_2[0, 4 * q : 4 * q + 4, :].bitcast(I32), o_s[32 * q : 32 * q + 4, :].bitcast(I32))

from contextlib import ExitStack

import concourse.mybir as mybir

F32 = mybir.dt.float32
BF16 = mybir.dt.bfloat16
I32 = mybir.dt.int32
U32 = mybir.dt.uint32
U16 = mybir.dt.uint16
U8 = mybir.dt.uint8
FP8X4 = mybir.dt.float8_e4m3fn_x4
FP4X4 = mybir.dt.float4_e2m1fn_x4
ALU = mybir.AluOpType
ACT = mybir.ActivationFunctionType

P = 128
T = 2048
S = 512
PACK = 4
QUADRANTS = 4
PER_COLUMN = 16
HALF = S // 2
VECTOR_SCATTER = 256
FUSED_HALVES = 2
FLOPS = 3 * 2 * S * S * S


def tile_picked_twocdsoftbrmssend_none_po_kernel(
    tc, x_words, x_scales, w1_words, w1_scales, gs, gs2, offs, n1, n2, n3, ca, cb, n4, n5, out_0, out_1, out_2
):
    nc = tc.nc
    with ExitStack() as ctx:
        held = ctx.enter_context(tc.tile_pool(name="held", bufs=1))
        psum = ctx.enter_context(tc.psum_pool(name="psum", bufs=1))

        def sbuf(name, width, dtype, tag=None):
            return held.tile([P, width], dtype, name=name, tag=tag or name, align_bytes=64)

        def load_list(name, src):
            tile = held.tile([P, S // PER_COLUMN], U16, name=name)
            nc.sync.dma_start(tile[:], src)
            return tile

        def entries(list_tile, cols):
            return list_tile[:, cols.start // PER_COLUMN : cols.stop // PER_COLUMN]

        def load_scale_rows(queues, tile, src):
            for q in range(QUADRANTS):
                queues[q].dma_start(tile[32 * q : 32 * q + 4, :].bitcast(I32), src[0, 4 * q : 4 * q + 4, :].bitcast(I32))

        def plane(tile, t, cols=slice(0, S)):
            return tile[:, S * t + cols.start : S * t + cols.stop]

        def deal_scales(dealt, plain):
            nc.vector.tensor_copy(
                dealt[:].rearrange("p (t m) -> p t m", t=PACK), plain[:].rearrange("p (m t) -> p t m", t=PACK)
            )

        def gather_scales(name, list_tile, tag):
            plain = sbuf(name + "_plain", S, U8, tag)
            dealt = sbuf(name, S, U8)
            nc.vector.tensor_copy(plain[:], x_s[:].indirect(list_tile[:]))
            deal_scales(dealt, plain)
            return dealt

        def gather_words(name, list_tile, tag):
            dealt = sbuf(name, S, U32, tag)
            nc.vector.tensor_copy(dealt[:].rearrange("p (t m) -> p m t", t=PACK), x_w[:].indirect(list_tile[:]))
            return dealt

        def weave(copy, woven, planes, cols):
            src = planes[:].rearrange("p (t c) -> p t c", t=PACK)[:, :, cols]
            dst = woven[:, PACK * cols.start : PACK * cols.stop]
            copy(dst.rearrange("p (c i t) -> p c t i", i=4, t=PACK), src.rearrange("p t (c i) -> p c t i", i=4))

        def quantise(name, woven):
            words = sbuf(name + "_w", S, U32)
            scales = sbuf(name + "_s", S, U8)
            nc.vector.quantize_mx(out=words[:].bitcast(FP8X4), scales=scales[:], in_=woven[:])
            return words, scales

        def product(banks, lhs_slices, lhs_scales, rhs_words, rhs_scales):
            for t in range(PACK):
                nc.tensor.matmul_mx(
                    out=banks[t][:],
                    lhsT=lhs_slices[t],
                    lhsT_scale=lhs_scales[:, P * t : P * (t + 1)],
                    rhs=rhs_words[:].bitcast(FP8X4),
                    rhs_scale=rhs_scales[:],
                    start=True,
                    stop=True,
                )

        def fp8_slices(words):
            return [words[:, P * t : P * (t + 1)].bitcast(FP8X4) for t in range(PACK)]

        halves = [slice(0, HALF), slice(HALF, S)]

        x_w = sbuf("x_w", T, U32)
        x_s = sbuf("x_s", T, U8)
        w_w = sbuf("w_w", 2 * S, U8)
        w_s = sbuf("w_s", S, U8)
        nc.gpsimd.memset(x_s[:].bitcast(I32), 0)
        nc.vector.memset(w_s[:].bitcast(I32), 0)
        l_offs = load_list("l_offs", offs)
        nc.scalar.dma_start(w_w[:].bitcast(I32), w1_words[0].bitcast(I32))
        nc.sync.dma_start(x_w[:].bitcast(I32), x_words[0].rearrange("p c r -> p (c r)").bitcast(I32))
        load_scale_rows([nc.scalar] * 4, x_s, x_scales)
        load_scale_rows([nc.sync, nc.sync, nc.sync, nc.gpsimd], w_s, w1_scales)
        l_cb = load_list("l_cb", cb)
        g1 = sbuf("g1", PACK, F32)
        g2 = sbuf("g2", PACK, F32)
        nc.gpsimd.dma_start(g2[:], gs2.rearrange("(p t) o -> p (t o)", t=PACK))
        l_n3 = load_list("l_n3", n3)
        l_ca = load_list("l_ca", ca)
        nc.gpsimd.dma_start(g1[:], gs.rearrange("(p t) o -> p (t o)", t=PACK))
        l_n1 = load_list("l_n1", n1)
        l_n2 = load_list("l_n2", n2)
        l_n5 = load_list("l_n5", n5)
        l_n4 = load_list("l_n4", n4)

        warm = sbuf("warm", 8, F32)
        nc.vector.memset(warm[:], 1.0)
        nc.scalar.activation(warm[:, 4:5], warm[:, 0:1], ACT.Abs_reciprocal_sqrt, bias=0.25)

        wd_w = sbuf("wd_w", 2 * S, U8)
        wd_s = sbuf("wd_s", S, U8)
        q_w = sbuf("q_w", S, U32)
        q_s = sbuf("q_s", S, U8)
        nc.vector.tensor_copy(
            wd_w[:].rearrange("p (t m e) -> p t m e", t=PACK, e=2), w_w[:].rearrange("p (m t e) -> p t m e", t=PACK, e=2)
        )
        nc.vector.tensor_copy(q_s[:], x_s[:].indirect(l_offs[:]))
        deal_scales(wd_s, w_s)
        nc.vector.tensor_copy(q_w[:], x_w[:].indirect(l_offs[:]))
        g2_half = sbuf("g2_half", PACK, F32)
        nc.gpsimd.tensor_scalar(g2_half[:], g2[:], -0.5, 0.0, ALU.mult, ALU.add)
        y = [psum.tile([P, S], F32, name=f"y{t}", tag=f"ya{t}") for t in range(PACK)]
        product(y, [wd_w[:, 2 * P * t : 2 * P * (t + 1)].bitcast(FP4X4) for t in range(PACK)], wd_s, q_w, q_s)

        sq_win = [sbuf(f"sq_win{t}", 2 * S, F32) for t in range(PACK)]
        y_win = [sbuf(f"y_win{t}", 2 * S, F32) for t in range(PACK)]
        sq_copy = sbuf("sq_copy", PACK * S, F32, "chain")
        for t in range(PACK):
            nc.scalar.activation(plane(sq_win[t], 0), y[t][:], ACT.Square)
            nc.vector.tensor_scalar(plane(sq_win[t], 1), y[t][:], 0.0, g2[:, t : t + 1], ALU.max, ALU.mult)
            nc.sync.dma_start(plane(sq_copy, t), plane(sq_win[t], 0))

        ds = [sbuf(f"ds{t}", S, F32) for t in range(PACK)]
        last = PACK - 1
        head, rest = slice(0, VECTOR_SCATTER), slice(VECTOR_SCATTER, S)
        nc.vector.tensor_copy(ds[last][:].indirect(entries(l_n3, head)), plane(sq_win[last], 1, head))
        cb_s = gather_scales("cb_s", l_cb, "cb_plain")
        ca_s = gather_scales("ca_s", l_ca, "g2")
        cb_w = gather_words("cb_w", l_cb, "cb_w")
        ca_w = gather_words("ca_w", l_ca, "q_w")
        for t, cols in [(t, cols) for cols in halves for t in range(last)] + [(last, rest)]:
            nc.scalar.activation(ds[t][:].indirect(entries(l_n3, cols)), plane(sq_win[t], 1, cols), ACT.Copy)

        for t in range(PACK):
            nc.vector.tensor_tensor(plane(y_win[t], 1), sq_win[t][:].indirect(l_n1[:]), plane(sq_copy, t), ALU.add)

        z2 = sbuf("z2", PACK * S, BF16, "chain")
        for t in range(PACK):
            nc.vector.scalar_tensor_tensor(plane(z2, t), y[t][:], g2_half[:, t : t + 1], ds[t][:], ALU.mult, ALU.add)
        inv_root = sbuf("inv_root", PACK * S, F32)
        for t in range(PACK):
            nc.scalar.activation(plane(inv_root, t), plane(y_win[t], 1), ACT.Abs_reciprocal_sqrt, bias=0.25)
        for t in range(PACK):
            nc.scalar.activation(plane(y_win[t], 0), y[t][:], ACT.Copy, scale=g1[:, t : t + 1])

        z2_woven = sbuf("z2_woven", PACK * S, BF16)
        weave(nc.vector.tensor_copy, z2_woven, z2, slice(0, S))
        z2_w, z2_s = quantise("z2", z2_woven)
        b = [psum.tile([P, S], F32, name=f"b{t}") for t in range(PACK)]
        product(b, fp8_slices(cb_w), cb_s, z2_w, z2_s)

        z = sbuf("z", PACK * S, F32, "chain")
        for t in range(PACK):
            nc.vector.tensor_tensor(plane(z, t), y_win[t][:].indirect(l_n2[:]), plane(inv_root, t), ALU.mult)
        tanh_b = sbuf("tanh_b", PACK * S, F32)
        z_woven = sbuf("z_woven", PACK * S, BF16)
        weave(nc.vector.tensor_copy, z_woven, z, slice(0, S))
        for t in range(PACK):
            nc.scalar.activation(plane(y_win[t], 0), b[t][:], ACT.Copy, scale=0.0625)
            nc.scalar.activation(plane(tanh_b, t), b[t][:], ACT.Tanh, scale=0.0625)
        z_w, z_s = quantise("z", z_woven)
        a = [psum.tile([P, S], F32, name=f"a{t}", tag=f"ya{t}") for t in range(PACK)]
        product(a, fp8_slices(ca_w), ca_s, z_w, z_s)

        a_win = [sbuf(f"a_win{t}", S, F32) for t in range(PACK)]
        tanh_b_prod = sbuf("tanh_b_prod", PACK * S, F32, "chain")
        result = sbuf("result", PACK * S, F32)
        for t in range(PACK):
            nc.scalar.activation(a_win[t][:], a[t][:], ACT.Copy, scale=0.0625)
        for t in range(PACK):
            nc.vector.tensor_tensor(plane(tanh_b_prod, t), y_win[t][:].indirect(l_n5[:]), plane(tanh_b, t), ALU.mult)

        out_rows = out_0.rearrange("(p t) j -> p t j", t=PACK)
        o_w = sbuf("o_w", S, U32)
        o_s = sbuf("o_s", S, U8)
        a_picked = sbuf("a_picked", PACK * S, F32)
        for h, cols in enumerate(halves):
            for t in range(PACK):
                picked = a_win[t][:].indirect(entries(l_n4, cols))
                if PACK * h + t >= FUSED_HALVES:
                    nc.scalar.activation(plane(a_picked, t, cols), picked, ACT.Copy)
                    picked = plane(a_picked, t, cols)
                nc.vector.tensor_tensor(plane(result, t, cols), picked, plane(tanh_b_prod, t, cols), ALU.subtract)
                nc.sync.dma_start(out_rows[:, t, cols], plane(result, t, cols))

        o_woven = sbuf("o_woven", PACK * S, BF16)
        weave(nc.scalar.copy, o_woven, result, halves[0])
        weave(nc.vector.tensor_copy, o_woven, result, halves[1])
        for cols in halves:
            nc.vector.quantize_mx(
                out=o_w[:, cols].bitcast(FP8X4), scales=o_s[:, cols], in_=o_woven[:, PACK * cols.start : PACK * cols.stop]
            )
            nc.sync.dma_start(out_1[0, :, cols, :].rearrange("p c r -> p (c r)").bitcast(I32), o_w[:, cols].bitcast(I32))
        for q, queue in enumerate([nc.scalar, nc.scalar, nc.scalar, nc.sync]):
            queue.dma_start(out_2[0, 4 * q : 4 * q + 4, :].bitcast(I32), o_s[32 * q : 32 * q + 4, :].bitcast(I32))
